import numpy as np
import ml_dtypes


def mxq(x, axis, fmt="e4m3"):
    dtype, down = {"e4m3": (ml_dtypes.float8_e4m3fn, 7), "e5m2": (ml_dtypes.float8_e5m2, 14)}[fmt]
    v = np.moveaxis(np.asarray(x, np.float32).astype(ml_dtypes.bfloat16).astype(np.float64), axis, -1)
    blocks = v.reshape(v.shape[:-1] + (-1, 32))
    amax = np.abs(blocks).max(-1, keepdims=True)
    byte = np.maximum(np.where(amax > 0, np.frexp(amax)[1] - 1 + 127, 0) - down, 1)
    scale = np.exp2(byte - 127.0)
    codes = (blocks / scale).astype(np.float32).astype(dtype).astype(np.float64)
    return np.moveaxis((codes * scale).reshape(v.shape), -1, axis)


WIDE = False


def mx_kscale(k):
    if not WIDE:
        return np.ones(k)
    levels = np.array([30, -30])
    if k % 512:
        return np.exp2(np.random.permutation(np.resize(levels, k // 32))).repeat(32)
    a = np.empty((k // 512, 16))
    for p in range(k // 512):
        a[p, :8] = np.random.permutation(np.resize(levels, 8))
        for g in range(8):
            far = levels[np.abs(levels - a[p, g]) >= 10]
            a[p, g + 8] = far[np.random.randint(len(far))]
    return np.exp2(a.ravel()).repeat(32)


def f64(x):
    return np.asarray(x).astype(np.float64)


def striped(idx):
    return np.tile(np.asarray(idx).reshape(-1, 16).T, (8, 1)).astype(np.uint16)


def unstriped(offs):
    return offs[:16].T.reshape(-1).astype(np.int64)


K, N, T, J = 512, 512, 2048, 512


def setup_inputs():
    n = np.random.standard_normal
    idx = np.random.permutation(T)[:J]
    fj = mx_kscale(J)
    return {
        "xa": (n((K, T))).astype(np.float32),
        "xb": (n((N, T))).astype(np.float32),
        "ra": (np.random.uniform(0.5, 1.5, (1, J)) * fj).astype(np.float32),
        "rb": (np.random.uniform(0.5, 1.5, (1, J)) / fj).astype(np.float32),
        "offs": striped(idx),
    }


def reference(xa, xb, ra, rb, offs):
    idx = unstriped(offs)
    da = (f64(xa)[:, idx] - np.mean(f64(xa)[:, idx], axis=1, keepdims=True)) * f64(ra)
    db = (f64(xb)[:, idx] - np.mean(f64(xb)[:, idx], axis=1, keepdims=True)) * f64(rb)
    ta = da.T
    tb = db.T
    taq = mxq(ta, 0, "e4m3")
    tbq = mxq(tb, 0, "e5m2")
    v = taq.T @ tbq
    y = 0.04 * v
    return y

@@ -1,0 +1,129 @@
+from contextlib import ExitStack
+
+import concourse.mybir as mybir
+from concourse.masks import make_identity
+
+K, N, T, J = 512, 512, 2048, 512
+FLOPS = 2 * K * N * J
+
+F32 = mybir.dt.float32
+BF16 = mybir.dt.bfloat16
+U32 = mybir.dt.uint32
+U16 = mybir.dt.uint16
+U8 = mybir.dt.uint8
+E4M3 = mybir.dt.float8_e4m3fn_x4
+E5M2 = mybir.dt.float8_e5m2_x4
+IDENTITY = mybir.ActivationFunctionType.Identity
+ADD = mybir.AluOpType.add
+MULT = mybir.AluOpType.mult
+
+P = 128
+HALF = J // 2
+OUT_SCALE = 0.04
+
+
+def tile_list_listed_cross_covariance_kernel(tc, xa, xb, ra, rb, offs, out):
+    nc = tc.nc
+    nb, na = N // P, K // P
+    sources = [xb[P * i : P * (i + 1), :] for i in range(nb)] + [xa[P * i : P * (i + 1), :] for i in range(na)]
+
+    with ExitStack() as ctx:
+        keep = ctx.enter_context(tc.tile_pool(name="keep", bufs=1))
+        rows = ctx.enter_context(tc.tile_pool(name="rows", bufs=1))
+        work = ctx.enter_context(tc.tile_pool(name="work", bufs=3))
+        psum_r = ctx.enter_context(tc.psum_pool(name="psum_r", bufs=2))
+        psum_t = ctx.enter_context(tc.psum_pool(name="psum_t", bufs=2))
+        psum_o = ctx.enter_context(tc.psum_pool(name="psum_o", bufs=2))
+
+        offsets = keep.tile([P, J // 16], U16, name="offsets")
+        windows = [rows.tile([P, T], F32, name="x%d" % i, tag="x%d" % i, align_bytes=64) for i in range(nb + na)]
+        nc.sync.dma_start(windows[0][:], sources[0])
+        nc.sync.dma_start(offsets[:], offs)
+        for i in range(1, nb + na):
+            nc.sync.dma_start(windows[i][:], sources[i])
+
+        ident = keep.tile([P, P], F32, name="ident")
+        make_identity(nc, ident[:])
+
+        weights = []
+        for name, r in (("rb", rb), ("ra", ra)):
+            r_cols = keep.tile([P, 4], F32, name=name + "_cols")
+            nc.scalar.dma_start(r_cols[:], r.rearrange("o (p t) -> (o p) t", t=4))
+            r_bank = psum_r.tile([P, 4, P], F32, name="r_bank")
+            for t in range(4):
+                nc.tensor.transpose(r_bank[:, t, :], r_cols[:, t : t + 1].to_broadcast([P, P]), ident[:])
+            r_all = keep.tile([P, J], F32, name=name + "_all")
+            nc.scalar.activation(
+                r_all[:].rearrange("p (n t) -> p n t", t=4), r_bank[:].rearrange("p t n -> p n t"), IDENTITY
+            )
+            weights.append(r_all)
+
+        b_grouped = keep.tile([P, N, 4], BF16, name="b_grouped", align_bytes=64)
+        b_codes = keep.tile([P, N], U32, name="b_codes", align_bytes=64)
+        unread = keep.tile([P, HALF], F32, name="unread")
+
+        def gather(i):
+            picked = work.tile([P, J], F32, name="picked", align_bytes=64)
+            sums = work.tile([P, 2], F32, name="sums")
+            for h in range(2):
+                cols = slice(h * HALF, (h + 1) * HALF)
+                nc.vector.tensor_copy(picked[:, cols], windows[i][:].indirect(offsets[:, h * HALF // 16 : (h + 1) * HALF // 16]))
+            nc.scalar.activation(unread[:], picked[:, 0:HALF], IDENTITY, scale=-1.0 / (J * HALF), accum_out=sums[:, 0:1])
+            nc.scalar.activation(
+                unread[:], picked[:, HALF:J], IDENTITY, bias=sums[:, 0:1], scale=-1.0 / J, accum_out=sums[:, 1:2]
+            )
+            return picked, sums
+
+        def centre_and_turn(picked, sums, r_all, grouped):
+            bank = psum_t.tile([P, 2, P], F32, name="bank")
+            for u in range(2):
+                centred = work.tile([P, HALF], BF16, name="centred%d" % u, align_bytes=64)
+                nc.vector.scalar_tensor_tensor(
+                    centred[:].rearrange("p (b i) -> p b i", i=16),
+                    picked[:].rearrange("p (b u i) -> p u b i", u=2, i=16)[:, u],
+                    sums[:, 1:2],
+                    r_all[:].rearrange("p (b u i) -> p u b i", u=2, i=16)[:, u],
+                    ADD,
+                    MULT,
+                )
+                nc.tensor.transpose(bank[:, u, :], centred[:].bitcast(F32), ident[:])
+            nc.scalar.copy(
+                grouped.rearrange("p k t -> p (k t)").bitcast(F32).rearrange("p (k u) -> p k u", u=2),
+                bank[:].rearrange("p u k -> p k u"),
+            )
+
+        def multiply(m, grouped, scales, b_scales, on_vector):
+            codes = work.tile([P, P], U32, name="codes", align_bytes=64)
+            nc.vector.quantize_mx(codes[:].bitcast(E4M3), scales[:], grouped[:].rearrange("p k t -> p (k t)"))
+            acc = psum_o.tile([P, N], F32, name="acc")
+            nc.tensor.matmul_mx(
+                acc[:], lhsT=codes[:].bitcast(E4M3), lhsT_scale=scales[:],
+                rhs=b_codes[:].bitcast(E5M2), rhs_scale=b_scales[:], start=True, stop=True,
+            )
+            result = work.tile([P, N], F32, name="result")
+            if on_vector:
+                nc.vector.tensor_scalar(result[:], acc[:], OUT_SCALE, None, MULT)
+            else:
+                nc.scalar.activation(result[:], acc[:], IDENTITY, scale=OUT_SCALE)
+            nc.sync.dma_start(out[P * m : P * (m + 1), :], result[:])
+
+        for i in range(nb):
+            picked, sums = gather(i)
+            centre_and_turn(picked, sums, weights[0], b_grouped[:, P * i : P * (i + 1), :])
+
+        pending = None
+        for m in range(na):
+            i = nb + m
+            picked, sums = gather(i)
+            if m == 0:
+                b_scales = rows.tile([P, N], U8, name="b_scales", tag="x%d" % i, align_bytes=64)
+                nc.vector.quantize_mx(
+                    b_codes[:].bitcast(E5M2), b_scales[:], b_grouped[:].rearrange("p n t -> p (n t)")
+                )
+            else:
+                a_scales = rows.tile([P, P], U8, name="a_scales", tag="x%d" % i, align_bytes=64)
+                multiply(m - 1, pending, a_scales, b_scales, m == na - 1)
+            pending = work.tile([P, P, 4], BF16, name="a_grouped", align_bytes=64)
+            centre_and_turn(picked, sums, weights[1], pending[:])
+        last_scales = keep.tile([P, P], U8, name="last_scales", align_bytes=64)
+        multiply(na - 1, pending, last_scales, b_scales, False)

@@ -22,108 +22,165 @@ HALF = J // 2
 OUT_SCALE = 0.04
 
 
+WINDOW_BYTES = T * 4
+SLOT = 2048
+
+
 def tile_list_listed_cross_covariance_kernel(tc, xa, xb, ra, rb, offs, out):
     nc = tc.nc
     nb, na = N // P, K // P
+    last = nb + na - 1
     sources = [xb[P * i : P * (i + 1), :] for i in range(nb)] + [xa[P * i : P * (i + 1), :] for i in range(na)]
 
     with ExitStack() as ctx:
         keep = ctx.enter_context(tc.tile_pool(name="keep", bufs=1))
-        rows = ctx.enter_context(tc.tile_pool(name="rows", bufs=1))
-        work = ctx.enter_context(tc.tile_pool(name="work", bufs=3))
+        arena = ctx.enter_context(tc.tile_pool(name="arena", bufs=1))
+        work = ctx.enter_context(tc.tile_pool(name="work", bufs=4))
         psum_r = ctx.enter_context(tc.psum_pool(name="psum_r", bufs=2))
         psum_t = ctx.enter_context(tc.psum_pool(name="psum_t", bufs=2))
-        psum_o = ctx.enter_context(tc.psum_pool(name="psum_o", bufs=2))
+        psum_o = ctx.enter_context(tc.psum_pool(name="psum_o", bufs=4))
+
+        def place(name, shape, dtype, offset):
+            return arena.tile(shape, dtype, name=name, offset=offset, align_bytes=64)
+
+        def window_at(i):
+            return WINDOW_BYTES * i
+
+        unread_at = WINDOW_BYTES * (last + 1)
+        last_grouped_at = unread_at + SLOT
+
+        picked_at = last_grouped_at + SLOT
 
         offsets = keep.tile([P, J // 16], U16, name="offsets")
-        windows = [rows.tile([P, T], F32, name="x%d" % i, tag="x%d" % i, align_bytes=64) for i in range(nb + na)]
+        windows = [place("x%d" % i, [P, T], F32, window_at(i)) for i in range(last + 1)]
         nc.sync.dma_start(windows[0][:], sources[0])
         nc.sync.dma_start(offsets[:], offs)
-        for i in range(1, nb + na):
+        r_cols = []
+        for name, r in (("rb", rb), ("ra", ra)):
+            cols = keep.tile([P, 4], F32, name=name + "_cols")
+            nc.sync.dma_start(cols[:], r.rearrange("o (p t) -> (o p) t", t=4))
+            r_cols.append(cols)
+        for i in range(1, last + 1):
             nc.sync.dma_start(windows[i][:], sources[i])
 
         ident = keep.tile([P, P], F32, name="ident")
         make_identity(nc, ident[:])
 
         weights = []
-        for name, r in (("rb", rb), ("ra", ra)):
-            r_cols = keep.tile([P, 4], F32, name=name + "_cols")
-            nc.scalar.dma_start(r_cols[:], r.rearrange("o (p t) -> (o p) t", t=4))
+        for s in range(2):
             r_bank = psum_r.tile([P, 4, P], F32, name="r_bank")
             for t in range(4):
-                nc.tensor.transpose(r_bank[:, t, :], r_cols[:, t : t + 1].to_broadcast([P, P]), ident[:])
-            r_all = keep.tile([P, J], F32, name=name + "_all")
-            nc.scalar.activation(
-                r_all[:].rearrange("p (n t) -> p n t", t=4), r_bank[:].rearrange("p t n -> p n t"), IDENTITY
-            )
-            weights.append(r_all)
+                nc.tensor.transpose(r_bank[:, t, :], r_cols[s][:, t : t + 1].to_broadcast([P, P]), ident[:])
+            weights.append(r_bank[:].rearrange("p t n -> p n t"))
 
-        b_grouped = keep.tile([P, N, 4], BF16, name="b_grouped", align_bytes=64)
         b_codes = keep.tile([P, N], U32, name="b_codes", align_bytes=64)
-        unread = keep.tile([P, HALF], F32, name="unread")
+        b_scales = keep.tile([P, N], U8, name="b_scales", align_bytes=64)
+
+        picked, sums, banks, grouped, accs = {}, {}, {}, {}, {}
 
         def gather(i):
-            picked = work.tile([P, J], F32, name="picked", align_bytes=64)
-            sums = work.tile([P, 2], F32, name="sums")
-            for h in range(2):
-                cols = slice(h * HALF, (h + 1) * HALF)
-                nc.vector.tensor_copy(picked[:, cols], windows[i][:].indirect(offsets[:, h * HALF // 16 : (h + 1) * HALF // 16]))
-            nc.scalar.activation(unread[:], picked[:, 0:HALF], IDENTITY, scale=-1.0 / (J * HALF), accum_out=sums[:, 0:1])
-            nc.scalar.activation(
-                unread[:], picked[:, HALF:J], IDENTITY, bias=sums[:, 0:1], scale=-1.0 / J, accum_out=sums[:, 1:2]
-            )
-            return picked, sums
-
-        def centre_and_turn(picked, sums, r_all, grouped):
-            bank = psum_t.tile([P, 2, P], F32, name="bank")
-            for u in range(2):
-                centred = work.tile([P, HALF], BF16, name="centred%d" % u, align_bytes=64)
-                nc.vector.scalar_tensor_tensor(
-                    centred[:].rearrange("p (b i) -> p b i", i=16),
-                    picked[:].rearrange("p (b u i) -> p u b i", u=2, i=16)[:, u],
-                    sums[:, 1:2],
-                    r_all[:].rearrange("p (b u i) -> p u b i", u=2, i=16)[:, u],
-                    ADD,
-                    MULT,
+            picked[i] = place("picked%d" % i, [P, J], F32, picked_at + SLOT * (0 if i == 2 else i))
+            sums[i] = work.tile([P, 2], F32, name="sums")
+            unread = place("unread%d" % i, [P, J], F32, unread_at)
+            if i < last:
+                nc.vector.tensor_copy(picked[i][:], windows[i][:].indirect(offsets[:]))
+                if 0 <= i - 2 < nb:
+                    group(i - 2)
+                nc.scalar.activation(unread[:], picked[i][:], IDENTITY, scale=-1.0 / J, accum_out=sums[i][:, 1:2])
+            else:
+                for h in range(2):
+                    cols = slice(h * HALF, (h + 1) * HALF)
+                    nc.vector.tensor_copy(
+                        picked[i][:, cols], windows[i][:].indirect(offsets[:, h * HALF // 16 : (h + 1) * HALF // 16])
+                    )
+                nc.scalar.activation(
+                    unread[:, 0:HALF], picked[i][:, 0:HALF], IDENTITY, scale=-1.0 / (J * HALF), accum_out=sums[i][:, 0:1]
                 )
-                nc.tensor.transpose(bank[:, u, :], centred[:].bitcast(F32), ident[:])
+                nc.scalar.activation(
+                    unread[:, HALF:J], picked[i][:, HALF:J], IDENTITY, bias=sums[i][:, 0:1], scale=-1.0 / J,
+                    accum_out=sums[i][:, 1:2],
+                )
+
+        def centre(i):
+            banks[i] = psum_t.tile([P, 2, P], F32, name="bank")
+            values = picked[i][:].rearrange("p (n t) -> p n t", t=4)
+            at = window_at((i + 1) % (last + 1))
+            if i < last:
+                centred = place("centred%d" % i, [P, J], BF16, at)
+                nc.vector.scalar_tensor_tensor(
+                    centred[:].rearrange("p (n t) -> p n t", t=4), values, sums[i][:, 1:2], weights[i // nb], ADD, MULT
+                )
+                words = centred[:].bitcast(F32)
+                for u in range(2):
+                    nc.tensor.transpose(banks[i][:, u, :], words[:, u : 2 * P : 2], ident[:])
+            else:
+                for u in range(2):
+                    centred = place("centred%d_%d" % (i, u), [P, HALF], BF16, at + 512 * u)
+                    nc.vector.scalar_tensor_tensor(
+                        centred[:].rearrange("p (n e) -> p n e", e=2), values[:, :, 2 * u : 2 * u + 2],
+                        sums[i][:, 1:2], weights[i // nb][:, :, 2 * u : 2 * u + 2], ADD, MULT,
+                    )
+                    nc.tensor.transpose(banks[i][:, u, :], centred[:].bitcast(F32), ident[:])
+
+        def group(i):
+            if i < nb:
+                grouped[i] = place("grouped%d" % i, [P, 4 * P], BF16, window_at(i + 2) + 1024)
+            elif i == last:
+                grouped[i] = place("grouped%d" % i, [P, 4 * P], BF16, last_grouped_at)
+            else:
+                grouped[i] = work.tile([P, 4 * P], BF16, name="grouped", align_bytes=64)
             nc.scalar.copy(
-                grouped.rearrange("p k t -> p (k t)").bitcast(F32).rearrange("p (k u) -> p k u", u=2),
-                bank[:].rearrange("p u k -> p k u"),
+                grouped[i][:].bitcast(F32).rearrange("p (k u) -> p k u", u=2), banks[i][:].rearrange("p u k -> p k u")
             )
 
-        def multiply(m, grouped, scales, b_scales, on_vector):
-            codes = work.tile([P, P], U32, name="codes", align_bytes=64)
-            nc.vector.quantize_mx(codes[:].bitcast(E4M3), scales[:], grouped[:].rearrange("p k t -> p (k t)"))
-            acc = psum_o.tile([P, N], F32, name="acc")
+        def quantise_b(i):
+            cols = slice(P * i, P * (i + 1))
+            nc.vector.quantize_mx(b_codes[:, cols].bitcast(E5M2), b_scales[:, cols], grouped[i][:])
+
+        def multiply(i):
+            if i + 2 < last:
+                codes = place("codes%d" % i, [P, P], U32, window_at(i + 2) + 1024)
+            elif i + 2 == last:
+                codes = place("codes%d" % i, [P, P], U32, picked_at + SLOT * last)
+            else:
+                codes = work.tile([P, P], U32, name="codes", align_bytes=64)
+            scales = work.tile([P, P], U8, name="scales", align_bytes=64)
+            nc.vector.quantize_mx(codes[:].bitcast(E4M3), scales[:], grouped[i][:])
+            accs[i] = psum_o.tile([P, N], F32, name="acc")
             nc.tensor.matmul_mx(
-                acc[:], lhsT=codes[:].bitcast(E4M3), lhsT_scale=scales[:],
+                accs[i][:], lhsT=codes[:].bitcast(E4M3), lhsT_scale=scales[:],
                 rhs=b_codes[:].bitcast(E5M2), rhs_scale=b_scales[:], start=True, stop=True,
             )
-            result = work.tile([P, N], F32, name="result")
-            if on_vector:
-                nc.vector.tensor_scalar(result[:], acc[:], OUT_SCALE, None, MULT)
-            else:
-                nc.scalar.activation(result[:], acc[:], IDENTITY, scale=OUT_SCALE)
-            nc.sync.dma_start(out[P * m : P * (m + 1), :], result[:])
 
-        for i in range(nb):
-            picked, sums = gather(i)
-            centre_and_turn(picked, sums, weights[0], b_grouped[:, P * i : P * (i + 1), :])
+        def store(i, at, on_vector, pieces):
+            m = i - nb
+            width = N // pieces
+            for c in range(pieces):
+                cols = slice(c * width, (c + 1) * width)
+                result = place("result%d_%d" % (i, c), [P, width], F32, at + 4 * width * c)
+                if on_vector:
+                    nc.vector.tensor_scalar(result[:], accs[i][:, cols], OUT_SCALE, None, MULT)
+                else:
+                    nc.scalar.activation(result[:], accs[i][:, cols], IDENTITY, scale=OUT_SCALE)
+                nc.sync.dma_start(out[P * m : P * (m + 1), cols], result[:])
 
-        pending = None
-        for m in range(na):
-            i = nb + m
-            picked, sums = gather(i)
-            if m == 0:
-                b_scales = rows.tile([P, N], U8, name="b_scales", tag="x%d" % i, align_bytes=64)
-                nc.vector.quantize_mx(
-                    b_codes[:].bitcast(E5M2), b_scales[:], b_grouped[:].rearrange("p n t -> p (n t)")
-                )
-            else:
-                a_scales = rows.tile([P, P], U8, name="a_scales", tag="x%d" % i, align_bytes=64)
-                multiply(m - 1, pending, a_scales, b_scales, m == na - 1)
-            pending = work.tile([P, P, 4], BF16, name="a_grouped", align_bytes=64)
-            centre_and_turn(picked, sums, weights[1], pending[:])
-        last_scales = keep.tile([P, P], U8, name="last_scales", align_bytes=64)
-        multiply(na - 1, pending, last_scales, b_scales, False)
+        for i in range(last + 1):
+            gather(i)
+            if i >= 1:
+                centre(i - 1)
+            if 0 <= i - 2 < nb:
+                quantise_b(i - 2)
+            if nb <= i - 2 < last - 2:
+                multiply(i - 2)
+            if i - 1 >= nb and i < last:
+                group(i - 1)
+        store(last - 3, unread_at, False, 1)
+        centre(last)
+        multiply(last - 2)
+        group(last - 1)
+        multiply(last - 1)
+        group(last)
+        store(last - 2, window_at(0) + 512, False, 1)
+        multiply(last)
+        store(last - 1, last_grouped_at, True, 1)
+        store(last, window_at(1) + 4096, False, 2)

from contextlib import ExitStack

import concourse.mybir as mybir
from concourse.masks import make_identity

K, N, T, J = 512, 512, 2048, 512
FLOPS = 2 * K * N * J

F32 = mybir.dt.float32
BF16 = mybir.dt.bfloat16
U32 = mybir.dt.uint32
U16 = mybir.dt.uint16
U8 = mybir.dt.uint8
E4M3 = mybir.dt.float8_e4m3fn_x4
E5M2 = mybir.dt.float8_e5m2_x4
IDENTITY = mybir.ActivationFunctionType.Identity
ADD = mybir.AluOpType.add
MULT = mybir.AluOpType.mult

P = 128
HALF = J // 2
OUT_SCALE = 0.04


WINDOW_BYTES = T * 4
SLOT = 2048


def tile_list_listed_cross_covariance_kernel(tc, xa, xb, ra, rb, offs, out):
    nc = tc.nc
    nb, na = N // P, K // P
    last = nb + na - 1
    sources = [xb[P * i : P * (i + 1), :] for i in range(nb)] + [xa[P * i : P * (i + 1), :] for i in range(na)]

    with ExitStack() as ctx:
        keep = ctx.enter_context(tc.tile_pool(name="keep", bufs=1))
        arena = ctx.enter_context(tc.tile_pool(name="arena", bufs=1))
        work = ctx.enter_context(tc.tile_pool(name="work", bufs=4))
        psum_r = ctx.enter_context(tc.psum_pool(name="psum_r", bufs=2))
        psum_t = ctx.enter_context(tc.psum_pool(name="psum_t", bufs=2))
        psum_o = ctx.enter_context(tc.psum_pool(name="psum_o", bufs=4))

        def place(name, shape, dtype, offset):
            return arena.tile(shape, dtype, name=name, offset=offset, align_bytes=64)

        def window_at(i):
            return WINDOW_BYTES * i

        unread_at = WINDOW_BYTES * (last + 1)
        last_grouped_at = unread_at + SLOT

        picked_at = last_grouped_at + SLOT

        offsets = keep.tile([P, J // 16], U16, name="offsets")
        windows = [place("x%d" % i, [P, T], F32, window_at(i)) for i in range(last + 1)]
        nc.sync.dma_start(windows[0][:], sources[0])
        nc.sync.dma_start(offsets[:], offs)
        r_cols = []
        for name, r in (("rb", rb), ("ra", ra)):
            cols = keep.tile([P, 4], F32, name=name + "_cols")
            nc.sync.dma_start(cols[:], r.rearrange("o (p t) -> (o p) t", t=4))
            r_cols.append(cols)
        for i in range(1, last + 1):
            nc.sync.dma_start(windows[i][:], sources[i])

        ident = keep.tile([P, P], F32, name="ident")
        make_identity(nc, ident[:])

        weights = []
        for s in range(2):
            r_bank = psum_r.tile([P, 4, P], F32, name="r_bank")
            for t in range(4):
                nc.tensor.transpose(r_bank[:, t, :], r_cols[s][:, t : t + 1].to_broadcast([P, P]), ident[:])
            weights.append(r_bank[:].rearrange("p t n -> p n t"))

        b_codes = keep.tile([P, N], U32, name="b_codes", align_bytes=64)
        b_scales = keep.tile([P, N], U8, name="b_scales", align_bytes=64)

        picked, sums, banks, grouped, accs = {}, {}, {}, {}, {}

        def gather(i):
            picked[i] = place("picked%d" % i, [P, J], F32, picked_at + SLOT * (0 if i == 2 else i))
            sums[i] = work.tile([P, 2], F32, name="sums")
            unread = place("unread%d" % i, [P, J], F32, unread_at)
            if i < last:
                nc.vector.tensor_copy(picked[i][:], windows[i][:].indirect(offsets[:]))
                if 0 <= i - 2 < nb:
                    group(i - 2)
                nc.scalar.activation(unread[:], picked[i][:], IDENTITY, scale=-1.0 / J, accum_out=sums[i][:, 1:2])
            else:
                for h in range(2):
                    cols = slice(h * HALF, (h + 1) * HALF)
                    nc.vector.tensor_copy(
                        picked[i][:, cols], windows[i][:].indirect(offsets[:, h * HALF // 16 : (h + 1) * HALF // 16])
                    )
                nc.scalar.activation(
                    unread[:, 0:HALF], picked[i][:, 0:HALF], IDENTITY, scale=-1.0 / (J * HALF), accum_out=sums[i][:, 0:1]
                )
                nc.scalar.activation(
                    unread[:, HALF:J], picked[i][:, HALF:J], IDENTITY, bias=sums[i][:, 0:1], scale=-1.0 / J,
                    accum_out=sums[i][:, 1:2],
                )

        def centre(i):
            banks[i] = psum_t.tile([P, 2, P], F32, name="bank")
            values = picked[i][:].rearrange("p (n t) -> p n t", t=4)
            at = window_at((i + 1) % (last + 1))
            if i < last:
                centred = place("centred%d" % i, [P, J], BF16, at)
                nc.vector.scalar_tensor_tensor(
                    centred[:].rearrange("p (n t) -> p n t", t=4), values, sums[i][:, 1:2], weights[i // nb], ADD, MULT
                )
                words = centred[:].bitcast(F32)
                for u in range(2):
                    nc.tensor.transpose(banks[i][:, u, :], words[:, u : 2 * P : 2], ident[:])
            else:
                for u in range(2):
                    centred = place("centred%d_%d" % (i, u), [P, HALF], BF16, at + 512 * u)
                    nc.vector.scalar_tensor_tensor(
                        centred[:].rearrange("p (n e) -> p n e", e=2), values[:, :, 2 * u : 2 * u + 2],
                        sums[i][:, 1:2], weights[i // nb][:, :, 2 * u : 2 * u + 2], ADD, MULT,
                    )
                    nc.tensor.transpose(banks[i][:, u, :], centred[:].bitcast(F32), ident[:])

        def group(i):
            if i < nb:
                grouped[i] = place("grouped%d" % i, [P, 4 * P], BF16, window_at(i + 2) + 1024)
            elif i == last:
                grouped[i] = place("grouped%d" % i, [P, 4 * P], BF16, last_grouped_at)
            else:
                grouped[i] = work.tile([P, 4 * P], BF16, name="grouped", align_bytes=64)
            nc.scalar.copy(
                grouped[i][:].bitcast(F32).rearrange("p (k u) -> p k u", u=2), banks[i][:].rearrange("p u k -> p k u")
            )

        def quantise_b(i):
            cols = slice(P * i, P * (i + 1))
            nc.vector.quantize_mx(b_codes[:, cols].bitcast(E5M2), b_scales[:, cols], grouped[i][:])

        def multiply(i):
            if i + 2 < last:
                codes = place("codes%d" % i, [P, P], U32, window_at(i + 2) + 1024)
            elif i + 2 == last:
                codes = place("codes%d" % i, [P, P], U32, picked_at + SLOT * last)
            else:
                codes = work.tile([P, P], U32, name="codes", align_bytes=64)
            scales = work.tile([P, P], U8, name="scales", align_bytes=64)
            nc.vector.quantize_mx(codes[:].bitcast(E4M3), scales[:], grouped[i][:])
            accs[i] = psum_o.tile([P, N], F32, name="acc")
            nc.tensor.matmul_mx(
                accs[i][:], lhsT=codes[:].bitcast(E4M3), lhsT_scale=scales[:],
                rhs=b_codes[:].bitcast(E5M2), rhs_scale=b_scales[:], start=True, stop=True,
            )

        def store(i, at, on_vector, pieces):
            m = i - nb
            width = N // pieces
            for c in range(pieces):
                cols = slice(c * width, (c + 1) * width)
                result = place("result%d_%d" % (i, c), [P, width], F32, at + 4 * width * c)
                if on_vector:
                    nc.vector.tensor_scalar(result[:], accs[i][:, cols], OUT_SCALE, None, MULT)
                else:
                    nc.scalar.activation(result[:], accs[i][:, cols], IDENTITY, scale=OUT_SCALE)
                nc.sync.dma_start(out[P * m : P * (m + 1), cols], result[:])

        for i in range(last + 1):
            gather(i)
            if i >= 1:
                centre(i - 1)
            if 0 <= i - 2 < nb:
                quantise_b(i - 2)
            if nb <= i - 2 < last - 2:
                multiply(i - 2)
            if i - 1 >= nb and i < last:
                group(i - 1)
        store(last - 3, unread_at, False, 1)
        centre(last)
        multiply(last - 2)
        group(last - 1)
        multiply(last - 1)
        group(last)
        store(last - 2, window_at(0) + 512, False, 1)
        multiply(last)
        store(last - 1, last_grouped_at, True, 1)
        store(last, window_at(1) + 4096, False, 2)
